import numpy as np
import ml_dtypes


def mxq(x, axis, fmt="e4m3"):
    dtype, down = {"e4m3": (ml_dtypes.float8_e4m3fn, 7), "e5m2": (ml_dtypes.float8_e5m2, 14)}[fmt]
    v = np.moveaxis(np.asarray(x, np.float32).astype(ml_dtypes.bfloat16).astype(np.float64), axis, -1)
    blocks = v.reshape(v.shape[:-1] + (-1, 32))
    amax = np.abs(blocks).max(-1, keepdims=True)
    byte = np.maximum(np.where(amax > 0, np.frexp(amax)[1] - 1 + 127, 0) - down, 1)
    scale = np.exp2(byte - 127.0)
    codes = (blocks / scale).astype(np.float32).astype(dtype).astype(np.float64)
    return np.moveaxis((codes * scale).reshape(v.shape), -1, axis)


WIDE = False


def mx_kscale(k):
    if not WIDE:
        return np.ones(k)
    levels = np.array([10, -10, 5, -5, 0])
    if k % 512:
        return np.exp2(np.random.permutation(np.resize(levels, k // 32))).repeat(32)
    a = np.empty((k // 512, 16))
    for p in range(k // 512):
        a[p, :8] = np.random.permutation(np.resize(levels, 8))
        for g in range(8):
            far = levels[np.abs(levels - a[p, g]) >= 10]
            a[p, g + 8] = far[np.random.randint(len(far))]
    return np.exp2(a.ravel()).repeat(32)


def f64(x):
    return np.asarray(x).astype(np.float64)


def striped(idx):
    return np.tile(np.asarray(idx).reshape(-1, 16).T, (8, 1)).astype(np.uint16)


def unstriped(offs):
    return offs[:16].T.reshape(-1).astype(np.int64)


def striped8(idx):
    return np.asarray(idx).reshape(8, -1, 16).transpose(0, 2, 1).reshape(128, -1).astype(np.uint16)


def unstriped8(offs):
    return offs.reshape(8, 16, -1).transpose(0, 2, 1).reshape(8, -1).astype(np.int64)


def pick8(x, idx, run):
    r = np.arange(len(x))
    return x[r[:, None], idx[r % (8 * run) // run]]


E2M1 = np.array([0.0, 0.5, 1.0, 1.5, 2.0, 3.0, 4.0, 6.0, -0.0, -0.5, -1.0, -1.5, -2.0, -3.0, -4.0, -6.0])


def pack_weight(w, fmt):
    k, n = w.shape
    w = f64(np.asarray(w, np.float32).astype(ml_dtypes.bfloat16)).reshape(k // 32, 32, n)
    amax = np.abs(w).max(1)
    if fmt == "e4m3":
        byte = np.frexp(amax)[1] - 1 + 127 - 7
    else:
        mant, ex = np.frexp(amax / 6.0)
        byte = np.where(mant > 0.5, ex, ex - 1) + 127
    byte = np.clip(np.where(amax > 0, byte, 1), 1, 254)
    scaled = (w * np.exp2(127.0 - byte)[:, None, :]).reshape(k, n).astype(np.float32)
    by_word = np.ascontiguousarray(scaled.reshape(k // 512, 128, 4, n).transpose(0, 1, 3, 2))
    if fmt == "e4m3":
        words = by_word.astype(ml_dtypes.float8_e4m3fn).view(np.uint8)
    else:
        c = by_word.astype(ml_dtypes.float4_e2m1fn).view(np.uint8) & 0xF
        words = (c[..., 0::2] | (c[..., 1::2] << 4)).reshape(k // 512, 128, 2 * n)
    return np.ascontiguousarray(words), np.ascontiguousarray(byte.astype(np.uint8).reshape(k // 512, 16, n))


def unpack_weight(words, scales, fmt):
    g, _, n = scales.shape
    words = np.ascontiguousarray(words).reshape(g, 128, n, -1)
    if fmt == "e4m3":
        vals = words.view(ml_dtypes.float8_e4m3fn).astype(np.float64)
    else:
        nib = np.empty((g, 128, n, 4), np.uint8)
        nib[..., 0::2] = words & 0xF
        nib[..., 1::2] = words >> 4
        vals = E2M1[nib]
    vals = vals * np.repeat(np.exp2(scales.astype(np.float64) - 127.0), 8, axis=1)[..., None]
    return vals.transpose(0, 1, 3, 2).reshape(g * 512, n)


K, J, R, T, Z, M, O, N, U = 512, 512, 512, 2048, 512, 1024, 256, 256, 512


def setup_inputs():
    n = np.random.standard_normal
    idx = np.random.permutation(T)[:J]
    idx2 = np.random.permutation(M)[:J]
    idx3 = np.stack([np.random.permutation(J)[:O] for _ in range(8)])
    idx4 = np.stack([np.random.permutation(J)[:O] for _ in range(8)])
    idx5 = np.stack([np.random.permutation(U)[:O] for _ in range(8)])
    idx6 = np.stack([np.random.permutation(U)[:O] for _ in range(8)])
    fk = mx_kscale(K)
    fr = mx_kscale(R)
    fz = mx_kscale(Z)
    xtp = pack_weight(n((K, T)) * fk[:, None], "e2m1")
    wp = pack_weight(n((K, R)) * 1 / np.sqrt(K) / fk[:, None] * fr, "e4m3")
    xop = pack_weight(n((Z, M)) / fz[:, None], "e2m1")
    w2p = pack_weight(n((Z, R)) * 1 / np.sqrt(Z) * fz[:, None] * fr, "e4m3")
    wbp = pack_weight(n((R, N)) * 1 / np.sqrt(R) / fr[:, None], "e4m3")
    wop = pack_weight(n((R, N)) * 1 / np.sqrt(R) / fr[:, None], "e2m1")
    return {
        "xt_words": xtp[0],
        "xt_scales": xtp[1],
        "w_words": wp[0],
        "w_scales": wp[1],
        "xo_words": xop[0],
        "xo_scales": xop[1],
        "w2_words": w2p[0],
        "w2_scales": w2p[1],
        "sa": (np.random.uniform(0.5, 1.6, (R, 1))).astype(np.float32),
        "sb": (np.random.uniform(0.5, 1.6, (R, 1))).astype(np.float32),
        "wb_words": wbp[0],
        "wb_scales": wbp[1],
        "wo_words": wop[0],
        "wo_scales": wop[1],
        "offs": striped(idx),
        "offs2": striped(idx2),
        "offs3": striped8(idx3),
        "offs4": striped8(idx4),
        "offs5": striped8(idx5),
        "offs6": striped8(idx6),
    }


def reference(xt_words, xt_scales, w_words, w_scales, xo_words, xo_scales, w2_words, w2_scales, sa, sb, wb_words, wb_scales, wo_words, wo_scales, offs, offs2, offs3, offs4, offs5, offs6):
    idx = unstriped(offs)
    idx2 = unstriped(offs2)
    idx3 = unstriped8(offs3)
    idx4 = unstriped8(offs4)
    idx5 = unstriped8(offs5)
    idx6 = unstriped8(offs6)
    xtu = unpack_weight(xt_words, xt_scales, "e2m1")
    wu = unpack_weight(w_words, w_scales, "e4m3")
    xou = unpack_weight(xo_words, xo_scales, "e2m1")
    w2u = unpack_weight(w2_words, w2_scales, "e4m3")
    wbu = unpack_weight(wb_words, wb_scales, "e4m3")
    wou = unpack_weight(wo_words, wo_scales, "e2m1")
    xtidxg = xtu[:, idx]
    xoidx2g = xou[:, idx2]
    a = wu.T @ xtidxg + w2u.T @ xoidx2g
    hid = np.abs(pick8(a, idx3, 64) * f64(sa) - pick8(a, idx4, 64) * f64(sb))
    hidq = mxq(hid, 0, "e4m3")
    p = wbu.T @ hidq
    q = wou.T @ hidq
    m0 = np.zeros((N, U))
    m0[np.arange(N)[:, None], idx5[np.arange(N) % 128 // 16]] = p
    m1 = np.zeros((N, U))
    m1[np.arange(N)[:, None], idx6[np.arange(N) % 128 // 16]] = q
    y = m0 + m1
    return y

@@ -1,0 +1,209 @@
+from contextlib import ExitStack
+
+import concourse.mybir as mybir
+
+K, J, R, T, Z, M, O, N, U = 512, 512, 512, 2048, 512, 1024, 256, 256, 512
+FLOPS = 2 * (K * R * J + Z * R * J + 2 * R * N * O)
+
+F32 = mybir.dt.float32
+BF16 = mybir.dt.bfloat16
+I32 = mybir.dt.int32
+U32 = mybir.dt.uint32
+U16 = mybir.dt.uint16
+U8 = mybir.dt.uint8
+FP8X4 = mybir.dt.float8_e4m3fn_x4
+FP4X4 = mybir.dt.float4_e2m1fn_x4
+ALU = mybir.AluOpType
+COPY = mybir.ActivationFunctionType.Copy
+
+P = 128
+PACK = 4
+JH = J // 2
+OH = O // 2
+
+
+def tile_picked_tokens_plain_bank_grouppair_outcomes_twoposted_kernel(
+    tc, xt_words, xt_scales, w_words, w_scales, xo_words, xo_scales, w2_words, w2_scales,
+    sa, sb, wb_words, wb_scales, wo_words, wo_scales, offs, offs2, offs3, offs4, offs5, offs6, out,
+):
+    nc = tc.nc
+    with ExitStack() as ctx:
+        lists = ctx.enter_context(tc.tile_pool(name="lists", bufs=1))
+        pool = ctx.enter_context(tc.tile_pool(name="pool", bufs=1))
+        psum = ctx.enter_context(tc.psum_pool(name="psum", bufs=1))
+
+        def tile(name, shape, dtype, tag=None):
+            return pool.tile(shape, dtype, name=name, tag=tag or name, align_bytes=64)
+
+        def load_list(name, src):
+            t = lists.tile(list(src.shape), U16, name=name)
+            nc.sync.dma_start(t[:], src)
+            return t
+
+        def load_plane(queue, plane, scales):
+            for q in range(4):
+                queue.dma_start(plane[32 * q : 32 * q + 4, :].bitcast(I32), scales[0, 4 * q : 4 * q + 4, :].bitcast(I32))
+
+        def load_rows(name, scales):
+            width = scales.shape[2]
+            rows = tile(name, [4, 4, width], U8)
+            nc.sync.dma_start(rows[:].bitcast(I32), scales[0].rearrange("(q i) c -> i q c", q=4).bitcast(I32))
+            return rows
+
+        def spread(plane, rows):
+            for q in range(4):
+                nc.vector.tensor_copy(plane[32 * q : 32 * q + 4, :].bitcast(I32), rows[:, q, :].bitcast(I32))
+
+        xt_plane = tile("xt_plane", [P, T], U8)
+        nc.gpsimd.memset(xt_plane[:].bitcast(I32), 0)
+        xo_plane = tile("xo_plane", [P, M], U8)
+        w2_plane = tile("w2_plane", [P, R], U8)
+        w_plane = tile("w_plane", [P, R], U8)
+        for t in (xo_plane, w2_plane, w_plane):
+            nc.vector.memset(t[:].bitcast(I32), 0)
+
+        xo_rows = load_rows("xo_rows", xo_scales)
+        w2_rows = load_rows("w2_rows", w2_scales)
+        l2 = load_list("l2", offs2)
+        xo_win = tile("xo_win", [P, M], U16)
+        nc.sync.dma_start(xo_win[:].bitcast(I32), xo_words[0].bitcast(I32))
+        w_rows = load_rows("w_rows", w_scales)
+        w2_raw = tile("w2_raw", [P, R], U32)
+        nc.sync.dma_start(w2_raw[:].bitcast(I32), w2_words[0].rearrange("p n t -> p (n t)").bitcast(I32))
+        l1 = load_list("l1", offs)
+        xt_win = tile("xt_win", [P, T], U16)
+        nc.sync.dma_start(xt_win[:].bitcast(I32), xt_words[0].bitcast(I32))
+        w_raw = tile("w_raw", [P, R], U32)
+        nc.sync.dma_start(w_raw[:].bitcast(I32), w_words[0].rearrange("p n t -> p (n t)").bitcast(I32))
+        load_plane(nc.sync, xt_plane, xt_scales)
+        l3 = load_list("l3", offs3)
+        l4 = load_list("l4", offs4)
+        sa_sb = tile("sa_sb", [P, PACK], F32)
+        sb_sb = tile("sb_sb", [P, PACK], F32)
+        nc.sync.dma_start(sa_sb[:], sa.rearrange("(p t) o -> p (t o)", t=PACK))
+        nc.sync.dma_start(sb_sb[:], sb.rearrange("(p t) o -> p (t o)", t=PACK))
+        l5 = load_list("l5", offs5)
+        l6 = load_list("l6", offs6)
+
+        def deal(name, raw, plane, rows):
+            codes = tile(name + "_codes", [P, R], U32)
+            nc.scalar.copy(
+                codes[:].rearrange("p (t c i) -> p c t i", t=PACK, i=4),
+                raw[:].rearrange("p (c i t) -> p c t i", t=PACK, i=4),
+            )
+            spread(plane, rows)
+            dealt = tile(name + "_dealt", [P, R], U8)
+            nc.vector.tensor_copy(
+                dealt[:].rearrange("p (t m) -> p t m", t=PACK),
+                plane[:].rearrange("p (m t) -> p t m", t=PACK),
+            )
+            return codes, dealt
+
+        banks = [[psum.tile([P, JH], F32, name=f"a{t}{h}", tag=f"bank{2 * t + h}") for h in range(2)] for t in range(PACK)]
+
+        def a_pass(t, h, codes, plane, words, scale_ap, first):
+            nc.tensor.matmul_mx(
+                banks[t][h][:],
+                lhsT=codes[:, t * P : (t + 1) * P].bitcast(FP8X4),
+                lhsT_scale=plane[:, t * P : (t + 1) * P],
+                rhs=words[:, h * JH : (h + 1) * JH].bitcast(FP4X4),
+                rhs_scale=scale_ap,
+                start=first,
+                stop=not first,
+            )
+
+        spread(xo_plane, xo_rows)
+        xo_g = tile("xo_g", [P, J], U16)
+        nc.vector.tensor_copy(xo_g[:], xo_win[:].indirect(l2[:]))
+        xo_gs = tile("xo_gs", [P, J], U8)
+        nc.vector.tensor_copy(xo_gs[:], xo_plane[:].indirect(l2[:]))
+        w2_codes, w2_dealt = deal("w2", w2_raw, w2_plane, w2_rows)
+        for t in range(PACK):
+            for h in range(2):
+                a_pass(t, h, w2_codes, w2_dealt, xo_g, xo_gs[:, h * JH : (h + 1) * JH], True)
+
+        xt_g = tile("xt_g", [P, J], U16)
+        nc.vector.tensor_copy(xt_g[:], xt_win[:].indirect(l1[:]))
+        w_codes, w_dealt = deal("w", w_raw, w_plane, w_rows)
+        xt_gs = [tile(f"xt_gs{h}", [P, JH], U8) for h in range(2)]
+        for h in range(2):
+            nc.vector.tensor_copy(xt_gs[h][:], xt_plane[:].indirect(l1[:, h * JH // 16 : (h + 1) * JH // 16]))
+
+        a_sb = [tile(f"a_sb{t}", [P, J], F32) for t in range(PACK)]
+        for t, h in ((0, 0), (1, 0), (0, 1), (1, 1), (2, 0), (2, 1), (3, 0), (3, 1)):
+            a_pass(t, h, w_codes, w_dealt, xt_g, xt_gs[h][:], False)
+            dst = a_sb[t][:, h * JH : (h + 1) * JH]
+            if (t, h) in ((0, 0), (1, 0), (0, 1)):
+                nc.scalar.activation(dst, banks[t][h][:], COPY)
+            else:
+                nc.vector.tensor_copy(dst, banks[t][h][:])
+
+        wb_codes = tile("wb_codes", [P, N], U32, tag="w2_raw")
+        nc.sync.dma_start(wb_codes[:].bitcast(I32), wb_words[0].rearrange("p n t -> p (n t)").bitcast(I32))
+        wo_codes = tile("wo_codes", [P, N], U16, tag="w_raw")
+        nc.sync.dma_start(wo_codes[:].bitcast(I32), wo_words[0].bitcast(I32))
+        wb_plane = tile("wb_plane", [P, N], U8)
+        wo_plane = tile("wo_plane", [P, N], U8)
+        for t in (wb_plane, wo_plane):
+            nc.vector.memset(t[:].bitcast(I32), 0)
+        load_plane(nc.sync, wb_plane, wb_scales)
+        load_plane(nc.sync, wo_plane, wo_scales)
+
+        results = []
+        pages = []
+        for h in range(2):
+            cols = slice(h * OH // 16, (h + 1) * OH // 16)
+            if h == 0:
+                diff = tile("diff0", [P, PACK, OH], F32)
+                for t in range(PACK):
+                    ga = tile(f"ga{t}", [P, OH], F32)
+                    gb = tile(f"gb{t}", [P, OH], F32)
+                    nc.scalar.activation(ga[:], a_sb[t][:].indirect(l3[:, cols]), COPY, scale=sa_sb[:, t : t + 1])
+                    nc.scalar.activation(gb[:], a_sb[t][:].indirect(l4[:, cols]), COPY, scale=sb_sb[:, t : t + 1])
+                    nc.vector.tensor_tensor(diff[:, t, :], ga[:], gb[:], ALU.subtract)
+                for b in range(2):
+                    pages.append([tile(f"page{b}{s}", [P, U], F32, tag=("gb" if s else "ga") + str(b)) for s in range(2)])
+                    for s in range(2):
+                        nc.gpsimd.memset(pages[b][s][:], 0.0)
+            else:
+                late = tile("late", [P, 2, PACK * OH], F32, tag="ga2")
+                for t in range(PACK):
+                    part = slice(t * OH, (t + 1) * OH)
+                    nc.scalar.activation(late[:, 0, part], a_sb[t][:].indirect(l3[:, cols]), COPY, scale=sa_sb[:, t : t + 1])
+                    nc.scalar.activation(late[:, 1, part], a_sb[t][:].indirect(l4[:, cols]), COPY, scale=sb_sb[:, t : t + 1])
+                diff = tile("diff1", [P, PACK, OH], F32, tag="hid_codes0")
+                nc.vector.tensor_tensor(diff[:].rearrange("p t o -> p (t o)"), late[:, 0, :], late[:, 1, :], ALU.subtract)
+            hid = tile(f"hid{h}", [P, OH * PACK], BF16)
+            woven = diff[:].rearrange("p t o -> p o t")
+            nc.vector.scalar_tensor_tensor(
+                hid[:].rearrange("p (o t) -> p o t", t=PACK), woven, -1.0, woven, ALU.mult, ALU.max
+            )
+            codes = tile(f"hid_codes{h}", [P, OH], U32)
+            plane = tile(f"hid_plane{h}", [P, OH], U8)
+            nc.vector.quantize_mx(codes[:].bitcast(FP8X4), plane[:], hid[:])
+            for b in range(2):
+                for s in range(2):
+                    rows = slice(b * P, (b + 1) * P)
+                    bank = psum.tile([P, OH], F32, name=f"o{h}{b}{s}", tag=f"bank{4 * h + 2 * b + s}")
+                    nc.tensor.matmul_mx(
+                        bank[:],
+                        lhsT=wo_codes[:, rows].bitcast(FP4X4) if s else wb_codes[:, rows].bitcast(FP8X4),
+                        lhsT_scale=(wo_plane if s else wb_plane)[:, rows],
+                        rhs=codes[:].bitcast(FP8X4),
+                        rhs_scale=plane[:],
+                        start=True,
+                        stop=True,
+                    )
+                    res = tile(f"res{h}{b}{s}", [P, OH], F32)
+                    nc.vector.tensor_copy(res[:], bank[:])
+                    results.append((h, b, s, res))
+
+        for h, b, s, res in results:
+            cols = slice(h * OH // 16, (h + 1) * OH // 16)
+            nc.scalar.activation(pages[b][s][:].indirect((l6 if s else l5)[:, cols]), res[:], COPY)
+            if h == 1 and s == 1:
+                for c in range(2):
+                    part = slice(c * U // 2, (c + 1) * U // 2)
+                    y = tile(f"y{b}{c}", [P, U // 2], F32)
+                    nc.vector.tensor_tensor(y[:], pages[b][0][:, part], pages[b][1][:, part], ALU.add)
+                    nc.sync.dma_start(out[b * P : (b + 1) * P, part], y[:])

@@ -45,14 +45,9 @@ def tile_picked_tokens_plain_bank_grouppair_outcomes_twoposted_kernel(
                 queue.dma_start(plane[32 * q : 32 * q + 4, :].bitcast(I32), scales[0, 4 * q : 4 * q + 4, :].bitcast(I32))
 
         def load_rows(name, scales):
-            width = scales.shape[2]
-            rows = tile(name, [4, 4, width], U8)
+            rows = tile(name, [4, 4, R], U8)
             nc.sync.dma_start(rows[:].bitcast(I32), scales[0].rearrange("(q i) c -> i q c", q=4).bitcast(I32))
             return rows
-
-        def spread(plane, rows):
-            for q in range(4):
-                nc.vector.tensor_copy(plane[32 * q : 32 * q + 4, :].bitcast(I32), rows[:, q, :].bitcast(I32))
 
         xt_plane = tile("xt_plane", [P, T], U8)
         nc.gpsimd.memset(xt_plane[:].bitcast(I32), 0)
@@ -62,20 +57,20 @@ def tile_picked_tokens_plain_bank_grouppair_outcomes_twoposted_kernel(
         for t in (xo_plane, w2_plane, w_plane):
             nc.vector.memset(t[:].bitcast(I32), 0)
 
-        xo_rows = load_rows("xo_rows", xo_scales)
         w2_rows = load_rows("w2_rows", w2_scales)
-        l2 = load_list("l2", offs2)
         xo_win = tile("xo_win", [P, M], U16)
         nc.sync.dma_start(xo_win[:].bitcast(I32), xo_words[0].bitcast(I32))
-        w_rows = load_rows("w_rows", w_scales)
+        load_plane(nc.sync, xo_plane, xo_scales)
+        l2 = load_list("l2", offs2)
         w2_raw = tile("w2_raw", [P, R], U32)
         nc.sync.dma_start(w2_raw[:].bitcast(I32), w2_words[0].rearrange("p n t -> p (n t)").bitcast(I32))
-        l1 = load_list("l1", offs)
         xt_win = tile("xt_win", [P, T], U16)
         nc.sync.dma_start(xt_win[:].bitcast(I32), xt_words[0].bitcast(I32))
+        w_rows = load_rows("w_rows", w_scales)
         w_raw = tile("w_raw", [P, R], U32)
         nc.sync.dma_start(w_raw[:].bitcast(I32), w_words[0].rearrange("p n t -> p (n t)").bitcast(I32))
         load_plane(nc.sync, xt_plane, xt_scales)
+        l1 = load_list("l1", offs)
         l3 = load_list("l3", offs3)
         l4 = load_list("l4", offs4)
         sa_sb = tile("sa_sb", [P, PACK], F32)
@@ -85,59 +80,69 @@ def tile_picked_tokens_plain_bank_grouppair_outcomes_twoposted_kernel(
         l5 = load_list("l5", offs5)
         l6 = load_list("l6", offs6)
 
-        def deal(name, raw, plane, rows):
-            codes = tile(name + "_codes", [P, R], U32)
+        def deal_words(name, raw):
+            codes = tile(name, [P, R], U32)
             nc.scalar.copy(
                 codes[:].rearrange("p (t c i) -> p c t i", t=PACK, i=4),
                 raw[:].rearrange("p (c i t) -> p c t i", t=PACK, i=4),
             )
-            spread(plane, rows)
-            dealt = tile(name + "_dealt", [P, R], U8)
+            return codes
+
+        def deal_scales(name, plane, rows):
+            for q in range(4):
+                nc.vector.tensor_copy(plane[32 * q : 32 * q + 4, :].bitcast(I32), rows[:, q, :].bitcast(I32))
+            dealt = tile(name, [P, R], U8)
             nc.vector.tensor_copy(
                 dealt[:].rearrange("p (t m) -> p t m", t=PACK),
                 plane[:].rearrange("p (m t) -> p t m", t=PACK),
             )
-            return codes, dealt
+            return dealt
+
+        w2_dealt = deal_scales("w2_dealt", w2_plane, w2_rows)
+        w2_codes = deal_words("w2_codes", w2_raw)
+        w_codes = deal_words("w_codes", w_raw)
 
         banks = [[psum.tile([P, JH], F32, name=f"a{t}{h}", tag=f"bank{2 * t + h}") for h in range(2)] for t in range(PACK)]
 
-        def a_pass(t, h, codes, plane, words, scale_ap, first):
+        def a_pass(t, h, codes, plane, words, scale_bytes, first):
             nc.tensor.matmul_mx(
                 banks[t][h][:],
                 lhsT=codes[:, t * P : (t + 1) * P].bitcast(FP8X4),
                 lhsT_scale=plane[:, t * P : (t + 1) * P],
-                rhs=words[:, h * JH : (h + 1) * JH].bitcast(FP4X4),
-                rhs_scale=scale_ap,
+                rhs=words[:].bitcast(FP4X4),
+                rhs_scale=scale_bytes[:],
                 start=first,
                 stop=not first,
             )
 
-        spread(xo_plane, xo_rows)
-        xo_g = tile("xo_g", [P, J], U16)
-        nc.vector.tensor_copy(xo_g[:], xo_win[:].indirect(l2[:]))
-        xo_gs = tile("xo_gs", [P, J], U8)
-        nc.vector.tensor_copy(xo_gs[:], xo_plane[:].indirect(l2[:]))
-        w2_codes, w2_dealt = deal("w2", w2_raw, w2_plane, w2_rows)
-        for t in range(PACK):
-            for h in range(2):
-                a_pass(t, h, w2_codes, w2_dealt, xo_g, xo_gs[:, h * JH : (h + 1) * JH], True)
+        def gather(name, window, offsets, h, dtype):
+            picked = tile(f"{name}{h}", [P, JH], dtype)
+            nc.vector.tensor_copy(picked[:], window[:].indirect(offsets[:, h * JH // 16 : (h + 1) * JH // 16]))
+            return picked
 
-        xt_g = tile("xt_g", [P, J], U16)
-        nc.vector.tensor_copy(xt_g[:], xt_win[:].indirect(l1[:]))
-        w_codes, w_dealt = deal("w", w_raw, w_plane, w_rows)
-        xt_gs = [tile(f"xt_gs{h}", [P, JH], U8) for h in range(2)]
         for h in range(2):
-            nc.vector.tensor_copy(xt_gs[h][:], xt_plane[:].indirect(l1[:, h * JH // 16 : (h + 1) * JH // 16]))
+            xo_g = gather("xo_g", xo_win, l2, h, U16)
+            xo_gs = gather("xo_gs", xo_plane, l2, h, U8)
+            for t in range(PACK):
+                a_pass(t, h, w2_codes, w2_dealt, xo_g, xo_gs, True)
 
+        w_dealt = deal_scales("w_dealt", w_plane, w_rows)
         a_sb = [tile(f"a_sb{t}", [P, J], F32) for t in range(PACK)]
-        for t, h in ((0, 0), (1, 0), (0, 1), (1, 1), (2, 0), (2, 1), (3, 0), (3, 1)):
-            a_pass(t, h, w_codes, w_dealt, xt_g, xt_gs[h][:], False)
-            dst = a_sb[t][:, h * JH : (h + 1) * JH]
-            if (t, h) in ((0, 0), (1, 0), (0, 1)):
-                nc.scalar.activation(dst, banks[t][h][:], COPY)
-            else:
-                nc.vector.tensor_copy(dst, banks[t][h][:])
+        for h in range(2):
+            xt_g = gather("xt_g", xt_win, l1, h, U16)
+            xt_gs = gather("xt_gs", xt_plane, l1, h, U8)
+            for t in range(PACK):
+                a_pass(t, h, w_codes, w_dealt, xt_g, xt_gs, False)
+                dst = a_sb[t][:, h * JH : (h + 1) * JH]
+                if h == 0:
+                    nc.scalar.copy(dst, banks[t][h][:])
+                else:
+                    nc.vector.tensor_copy(dst, banks[t][h][:])
 
+        pages = [[tile(f"page{b}{s}", [P, U], F32) for s in range(2)] for b in range(2)]
+        for b in range(2):
+            for s in range(2):
+                nc.vector.memset(pages[b][s][:], 0.0)
         wb_codes = tile("wb_codes", [P, N], U32, tag="w2_raw")
         nc.sync.dma_start(wb_codes[:].bitcast(I32), wb_words[0].rearrange("p n t -> p (n t)").bitcast(I32))
         wo_codes = tile("wo_codes", [P, N], U16, tag="w_raw")
@@ -150,34 +155,26 @@ def tile_picked_tokens_plain_bank_grouppair_outcomes_twoposted_kernel(
         load_plane(nc.sync, wo_plane, wo_scales)
 
         results = []
-        pages = []
         for h in range(2):
             cols = slice(h * OH // 16, (h + 1) * OH // 16)
             if h == 0:
-                diff = tile("diff0", [P, PACK, OH], F32)
-                for t in range(PACK):
-                    ga = tile(f"ga{t}", [P, OH], F32)
-                    gb = tile(f"gb{t}", [P, OH], F32)
-                    nc.scalar.activation(ga[:], a_sb[t][:].indirect(l3[:, cols]), COPY, scale=sa_sb[:, t : t + 1])
-                    nc.scalar.activation(gb[:], a_sb[t][:].indirect(l4[:, cols]), COPY, scale=sb_sb[:, t : t + 1])
-                    nc.vector.tensor_tensor(diff[:, t, :], ga[:], gb[:], ALU.subtract)
-                for b in range(2):
-                    pages.append([tile(f"page{b}{s}", [P, U], F32, tag=("gb" if s else "ga") + str(b)) for s in range(2)])
-                    for s in range(2):
-                        nc.gpsimd.memset(pages[b][s][:], 0.0)
+                fetched = [[tile(f"g{u}{s}", [P, 2, OH], F32)[:] for s in range(2)] for u in range(2)]
             else:
-                late = tile("late", [P, 2, PACK * OH], F32, tag="ga2")
-                for t in range(PACK):
-                    part = slice(t * OH, (t + 1) * OH)
-                    nc.scalar.activation(late[:, 0, part], a_sb[t][:].indirect(l3[:, cols]), COPY, scale=sa_sb[:, t : t + 1])
-                    nc.scalar.activation(late[:, 1, part], a_sb[t][:].indirect(l4[:, cols]), COPY, scale=sb_sb[:, t : t + 1])
-                diff = tile("diff1", [P, PACK, OH], F32, tag="hid_codes0")
-                nc.vector.tensor_tensor(diff[:].rearrange("p t o -> p (t o)"), late[:, 0, :], late[:, 1, :], ALU.subtract)
+                late = tile("late", [P, 4, 2, OH], F32, tag="g00")
+                fetched = [[late[:, 2 * u + s] for s in range(2)] for u in range(2)]
             hid = tile(f"hid{h}", [P, OH * PACK], BF16)
-            woven = diff[:].rearrange("p t o -> p o t")
-            nc.vector.scalar_tensor_tensor(
-                hid[:].rearrange("p (o t) -> p o t", t=PACK), woven, -1.0, woven, ALU.mult, ALU.max
-            )
+            for u in range(2):
+                for e in range(2):
+                    t = 2 * u + e
+                    nc.scalar.activation(fetched[u][0][:, e, :], a_sb[t][:].indirect(l3[:, cols]), COPY, scale=sa_sb[:, t : t + 1])
+                    nc.scalar.activation(fetched[u][1][:, e, :], a_sb[t][:].indirect(l4[:, cols]), COPY, scale=sb_sb[:, t : t + 1])
+                diff = tile(f"diff{h}{u}", [P, OH, 2], F32, tag=("hid0", "hid_codes0")[u] if h else None)
+                nc.vector.tensor_tensor(
+                    diff[:], fetched[u][0].rearrange("p e o -> p o e"), fetched[u][1].rearrange("p e o -> p o e"), ALU.subtract
+                )
+                nc.vector.scalar_tensor_tensor(
+                    hid[:].rearrange("p (o u e) -> p o u e", u=2, e=2)[:, :, u, :], diff[:], -1.0, diff[:], ALU.mult, ALU.max
+                )
             codes = tile(f"hid_codes{h}", [P, OH], U32)
             plane = tile(f"hid_plane{h}", [P, OH], U8)
             nc.vector.quantize_mx(codes[:].bitcast(FP8X4), plane[:], hid[:])
@@ -206,4 +203,4 @@ def tile_picked_tokens_plain_bank_grouppair_outcomes_twoposted_kernel(
                     part = slice(c * U // 2, (c + 1) * U // 2)
                     y = tile(f"y{b}{c}", [P, U // 2], F32)
                     nc.vector.tensor_tensor(y[:], pages[b][0][:, part], pages[b][1][:, part], ALU.add)
-                    nc.sync.dma_start(out[b * P : (b + 1) * P, part], y[:])
+                    (nc.scalar if b == 1 and c == 1 else nc.sync).dma_start(out[b * P : (b + 1) * P, part], y[:])

@@ -44,33 +44,34 @@ def tile_picked_tokens_plain_bank_grouppair_outcomes_twoposted_kernel(
             for q in range(4):
                 queue.dma_start(plane[32 * q : 32 * q + 4, :].bitcast(I32), scales[0, 4 * q : 4 * q + 4, :].bitcast(I32))
 
-        def load_rows(name, scales):
-            rows = tile(name, [4, 4, R], U8)
-            nc.sync.dma_start(rows[:].bitcast(I32), scales[0].rearrange("(q i) c -> i q c", q=4).bitcast(I32))
-            return rows
+        def load_folded(folded, scales):
+            rows = scales[0].rearrange("(s u i) c -> u i s c", s=2, u=2)
+            for u in range(2):
+                nc.sync.dma_start(folded[32 * u : 32 * u + 4, :, :].bitcast(I32), rows[u].bitcast(I32))
 
-        xt_plane = tile("xt_plane", [P, T], U8)
-        nc.gpsimd.memset(xt_plane[:].bitcast(I32), 0)
         xo_plane = tile("xo_plane", [P, M], U8)
-        w2_plane = tile("w2_plane", [P, R], U8)
-        w_plane = tile("w_plane", [P, R], U8)
-        for t in (xo_plane, w2_plane, w_plane):
+        xt_plane = tile("xt_plane", [P, T], U8)
+        for t in (xo_plane, xt_plane):
+            nc.gpsimd.memset(t[:].bitcast(I32), 0)
+        w2_fold = tile("w2_fold", [P, 2, R], U8)
+        w_fold = tile("w_fold", [P, 2, R], U8)
+        for t in (w2_fold, w_fold):
             nc.vector.memset(t[:].bitcast(I32), 0)
 
-        w2_rows = load_rows("w2_rows", w2_scales)
         xo_win = tile("xo_win", [P, M], U16)
         nc.sync.dma_start(xo_win[:].bitcast(I32), xo_words[0].bitcast(I32))
-        load_plane(nc.sync, xo_plane, xo_scales)
         l2 = load_list("l2", offs2)
+        load_plane(nc.sync, xo_plane, xo_scales)
         w2_raw = tile("w2_raw", [P, R], U32)
         nc.sync.dma_start(w2_raw[:].bitcast(I32), w2_words[0].rearrange("p n t -> p (n t)").bitcast(I32))
         xt_win = tile("xt_win", [P, T], U16)
         nc.sync.dma_start(xt_win[:].bitcast(I32), xt_words[0].bitcast(I32))
-        w_rows = load_rows("w_rows", w_scales)
+        load_folded(w2_fold, w2_scales)
+        l1 = load_list("l1", offs)
         w_raw = tile("w_raw", [P, R], U32)
         nc.sync.dma_start(w_raw[:].bitcast(I32), w_words[0].rearrange("p n t -> p (n t)").bitcast(I32))
+        load_folded(w_fold, w_scales)
         load_plane(nc.sync, xt_plane, xt_scales)
-        l1 = load_list("l1", offs)
         l3 = load_list("l3", offs3)
         l4 = load_list("l4", offs4)
         sa_sb = tile("sa_sb", [P, PACK], F32)
@@ -88,17 +89,14 @@ def tile_picked_tokens_plain_bank_grouppair_outcomes_twoposted_kernel(
             )
             return codes
 
-        def deal_scales(name, plane, rows):
-            for q in range(4):
-                nc.vector.tensor_copy(plane[32 * q : 32 * q + 4, :].bitcast(I32), rows[:, q, :].bitcast(I32))
+        def deal_scales(name, folded):
+            nc.vector.tensor_copy(folded[64:128, 0, :].bitcast(I32), folded[0:64, 1, :].bitcast(I32))
             dealt = tile(name, [P, R], U8)
             nc.vector.tensor_copy(
-                dealt[:].rearrange("p (t m) -> p t m", t=PACK),
-                plane[:].rearrange("p (m t) -> p t m", t=PACK),
+                dealt[:].rearrange("p (t m) -> p t m", t=PACK), folded[:, 0, :].rearrange("p (m t) -> p t m", t=PACK)
             )
             return dealt
 
-        w2_dealt = deal_scales("w2_dealt", w2_plane, w2_rows)
         w2_codes = deal_words("w2_codes", w2_raw)
         w_codes = deal_words("w_codes", w_raw)
 
@@ -109,40 +107,43 @@ def tile_picked_tokens_plain_bank_grouppair_outcomes_twoposted_kernel(
                 banks[t][h][:],
                 lhsT=codes[:, t * P : (t + 1) * P].bitcast(FP8X4),
                 lhsT_scale=plane[:, t * P : (t + 1) * P],
-                rhs=words[:].bitcast(FP4X4),
-                rhs_scale=scale_bytes[:],
+                rhs=words[:, h * JH : (h + 1) * JH].bitcast(FP4X4),
+                rhs_scale=scale_bytes,
                 start=first,
                 stop=not first,
             )
 
-        def gather(name, window, offsets, h, dtype):
-            picked = tile(f"{name}{h}", [P, JH], dtype)
-            nc.vector.tensor_copy(picked[:], window[:].indirect(offsets[:, h * JH // 16 : (h + 1) * JH // 16]))
-            return picked
+        xo_g = tile("xo_g", [P, J], U16)
+        nc.vector.tensor_copy(xo_g[:], xo_win[:].indirect(l2[:]))
+        xo_gs = tile("xo_gs", [P, J], U8)
+        nc.vector.tensor_copy(xo_gs[:], xo_plane[:].indirect(l2[:]))
+        w2_dealt = deal_scales("w2_dealt", w2_fold)
 
+        def note_passes(t):
+            for h in range(2):
+                a_pass(t, h, w2_codes, w2_dealt, xo_g, xo_gs[:, h * JH : (h + 1) * JH], True)
+
+        for t in range(PACK - 1):
+            note_passes(t)
+
+        xt_g = tile("xt_g", [P, J], U16)
+        nc.vector.tensor_copy(xt_g[:], xt_win[:].indirect(l1[:]))
+        w_dealt = deal_scales("w_dealt", w_fold)
+        xt_gs = [tile(f"xt_gs{h}", [P, JH], U8) for h in range(2)]
         for h in range(2):
-            xo_g = gather("xo_g", xo_win, l2, h, U16)
-            xo_gs = gather("xo_gs", xo_plane, l2, h, U8)
-            for t in range(PACK):
-                a_pass(t, h, w2_codes, w2_dealt, xo_g, xo_gs, True)
+            nc.vector.tensor_copy(xt_gs[h][:], xt_plane[:].indirect(l1[:, h * JH // 16 : (h + 1) * JH // 16]))
 
-        w_dealt = deal_scales("w_dealt", w_plane, w_rows)
         a_sb = [tile(f"a_sb{t}", [P, J], F32) for t in range(PACK)]
-        for h in range(2):
-            xt_g = gather("xt_g", xt_win, l1, h, U16)
-            xt_gs = gather("xt_gs", xt_plane, l1, h, U8)
-            for t in range(PACK):
-                a_pass(t, h, w_codes, w_dealt, xt_g, xt_gs, False)
-                dst = a_sb[t][:, h * JH : (h + 1) * JH]
-                if h == 0:
-                    nc.scalar.copy(dst, banks[t][h][:])
-                else:
-                    nc.vector.tensor_copy(dst, banks[t][h][:])
+        for t, h in ((0, 0), (1, 0), (0, 1), (1, 1), (2, 0), (2, 1), (3, 0), (3, 1)):
+            if (t, h) == (PACK - 1, 0):
+                note_passes(t)
+            a_pass(t, h, w_codes, w_dealt, xt_g, xt_gs[h][:], False)
+            dst = a_sb[t][:, h * JH : (h + 1) * JH]
+            if (t, h) in ((0, 0), (1, 0)):
+                nc.scalar.copy(dst, banks[t][h][:])
+            else:
+                nc.vector.tensor_copy(dst, banks[t][h][:])
 
-        pages = [[tile(f"page{b}{s}", [P, U], F32) for s in range(2)] for b in range(2)]
-        for b in range(2):
-            for s in range(2):
-                nc.vector.memset(pages[b][s][:], 0.0)
         wb_codes = tile("wb_codes", [P, N], U32, tag="w2_raw")
         nc.sync.dma_start(wb_codes[:].bitcast(I32), wb_words[0].rearrange("p n t -> p (n t)").bitcast(I32))
         wo_codes = tile("wo_codes", [P, N], U16, tag="w_raw")
@@ -155,26 +156,36 @@ def tile_picked_tokens_plain_bank_grouppair_outcomes_twoposted_kernel(
         load_plane(nc.sync, wo_plane, wo_scales)
 
         results = []
+        pages = []
         for h in range(2):
             cols = slice(h * OH // 16, (h + 1) * OH // 16)
+            step = 1 + h
+            rows_abs = tile(f"rows_abs{h}", [P, PACK * OH], BF16)
+            if h == 1:
+                late = tile("late", [P, 2, PACK * OH], F32, tag="ga2")
+            for t0 in range(0, PACK, step):
+                part = slice(t0 * OH, (t0 + step) * OH)
+                if h == 0:
+                    ga = tile(f"ga{t0}", [P, OH], F32)[:]
+                    gb = tile(f"gb{t0}", [P, OH], F32)[:]
+                else:
+                    ga, gb = late[:, 0, part], late[:, 1, part]
+                for e in range(step):
+                    t = t0 + e
+                    nc.scalar.activation(ga[:, e * OH : (e + 1) * OH], a_sb[t][:].indirect(l3[:, cols]), COPY, scale=sa_sb[:, t : t + 1])
+                    nc.scalar.activation(gb[:, e * OH : (e + 1) * OH], a_sb[t][:].indirect(l4[:, cols]), COPY, scale=sb_sb[:, t : t + 1])
+                diff = tile(f"diff{h}{t0}", [P, step * OH], F32, tag=("hid0", "hid_codes0")[t0 // 2] if h else None)
+                nc.vector.tensor_tensor(diff[:], ga, gb, ALU.subtract)
+                nc.vector.scalar_tensor_tensor(rows_abs[:, part], diff[:], -1.0, diff[:], ALU.mult, ALU.max)
             if h == 0:
-                fetched = [[tile(f"g{u}{s}", [P, 2, OH], F32)[:] for s in range(2)] for u in range(2)]
-            else:
-                late = tile("late", [P, 4, 2, OH], F32, tag="g00")
-                fetched = [[late[:, 2 * u + s] for s in range(2)] for u in range(2)]
+                for b, tags in enumerate((("w_codes", "w_dealt"), ("ga0", "gb0"))):
+                    pages.append([tile(f"page{b}{s}", [P, U], F32, tag=tags[s]) for s in range(2)])
+                    for s in range(2):
+                        nc.gpsimd.memset(pages[b][s][:], 0.0)
             hid = tile(f"hid{h}", [P, OH * PACK], BF16)
-            for u in range(2):
-                for e in range(2):
-                    t = 2 * u + e
-                    nc.scalar.activation(fetched[u][0][:, e, :], a_sb[t][:].indirect(l3[:, cols]), COPY, scale=sa_sb[:, t : t + 1])
-                    nc.scalar.activation(fetched[u][1][:, e, :], a_sb[t][:].indirect(l4[:, cols]), COPY, scale=sb_sb[:, t : t + 1])
-                diff = tile(f"diff{h}{u}", [P, OH, 2], F32, tag=("hid0", "hid_codes0")[u] if h else None)
-                nc.vector.tensor_tensor(
-                    diff[:], fetched[u][0].rearrange("p e o -> p o e"), fetched[u][1].rearrange("p e o -> p o e"), ALU.subtract
-                )
-                nc.vector.scalar_tensor_tensor(
-                    hid[:].rearrange("p (o u e) -> p o u e", u=2, e=2)[:, :, u, :], diff[:], -1.0, diff[:], ALU.mult, ALU.max
-                )
+            nc.vector.tensor_copy(
+                hid[:].rearrange("p (c i t) -> p c t i", t=PACK, i=4), rows_abs[:].rearrange("p (t c i) -> p c t i", t=PACK, i=4)
+            )
             codes = tile(f"hid_codes{h}", [P, OH], U32)
             plane = tile(f"hid_plane{h}", [P, OH], U8)
             nc.vector.quantize_mx(codes[:].bitcast(FP8X4), plane[:], hid[:])

from contextlib import ExitStack

import concourse.mybir as mybir

K, J, R, T, Z, M, O, N, U = 512, 512, 512, 2048, 512, 1024, 256, 256, 512
FLOPS = 2 * (K * R * J + Z * R * J + 2 * R * N * O)

F32 = mybir.dt.float32
BF16 = mybir.dt.bfloat16
I32 = mybir.dt.int32
U32 = mybir.dt.uint32
U16 = mybir.dt.uint16
U8 = mybir.dt.uint8
FP8X4 = mybir.dt.float8_e4m3fn_x4
FP4X4 = mybir.dt.float4_e2m1fn_x4
ALU = mybir.AluOpType
COPY = mybir.ActivationFunctionType.Copy

P = 128
PACK = 4
JH = J // 2
OH = O // 2


def tile_picked_tokens_plain_bank_grouppair_outcomes_twoposted_kernel(
    tc, xt_words, xt_scales, w_words, w_scales, xo_words, xo_scales, w2_words, w2_scales,
    sa, sb, wb_words, wb_scales, wo_words, wo_scales, offs, offs2, offs3, offs4, offs5, offs6, out,
):
    nc = tc.nc
    with ExitStack() as ctx:
        lists = ctx.enter_context(tc.tile_pool(name="lists", bufs=1))
        pool = ctx.enter_context(tc.tile_pool(name="pool", bufs=1))
        psum = ctx.enter_context(tc.psum_pool(name="psum", bufs=1))

        def tile(name, shape, dtype, tag=None):
            return pool.tile(shape, dtype, name=name, tag=tag or name, align_bytes=64)

        def load_list(name, src):
            t = lists.tile(list(src.shape), U16, name=name)
            nc.sync.dma_start(t[:], src)
            return t

        def load_plane(queue, plane, scales):
            for q in range(4):
                queue.dma_start(plane[32 * q : 32 * q + 4, :].bitcast(I32), scales[0, 4 * q : 4 * q + 4, :].bitcast(I32))

        def load_folded(folded, scales):
            rows = scales[0].rearrange("(s u i) c -> u i s c", s=2, u=2)
            for u in range(2):
                nc.sync.dma_start(folded[32 * u : 32 * u + 4, :, :].bitcast(I32), rows[u].bitcast(I32))

        xo_plane = tile("xo_plane", [P, M], U8)
        xt_plane = tile("xt_plane", [P, T], U8)
        for t in (xo_plane, xt_plane):
            nc.gpsimd.memset(t[:].bitcast(I32), 0)
        w2_fold = tile("w2_fold", [P, 2, R], U8)
        w_fold = tile("w_fold", [P, 2, R], U8)
        for t in (w2_fold, w_fold):
            nc.vector.memset(t[:].bitcast(I32), 0)

        xo_win = tile("xo_win", [P, M], U16)
        nc.sync.dma_start(xo_win[:].bitcast(I32), xo_words[0].bitcast(I32))
        l2 = load_list("l2", offs2)
        load_plane(nc.sync, xo_plane, xo_scales)
        w2_raw = tile("w2_raw", [P, R], U32)
        nc.sync.dma_start(w2_raw[:].bitcast(I32), w2_words[0].rearrange("p n t -> p (n t)").bitcast(I32))
        xt_win = tile("xt_win", [P, T], U16)
        nc.sync.dma_start(xt_win[:].bitcast(I32), xt_words[0].bitcast(I32))
        load_folded(w2_fold, w2_scales)
        l1 = load_list("l1", offs)
        w_raw = tile("w_raw", [P, R], U32)
        nc.sync.dma_start(w_raw[:].bitcast(I32), w_words[0].rearrange("p n t -> p (n t)").bitcast(I32))
        load_folded(w_fold, w_scales)
        load_plane(nc.sync, xt_plane, xt_scales)
        l3 = load_list("l3", offs3)
        l4 = load_list("l4", offs4)
        sa_sb = tile("sa_sb", [P, PACK], F32)
        sb_sb = tile("sb_sb", [P, PACK], F32)
        nc.sync.dma_start(sa_sb[:], sa.rearrange("(p t) o -> p (t o)", t=PACK))
        nc.sync.dma_start(sb_sb[:], sb.rearrange("(p t) o -> p (t o)", t=PACK))
        l5 = load_list("l5", offs5)
        l6 = load_list("l6", offs6)

        def deal_words(name, raw):
            codes = tile(name, [P, R], U32)
            nc.scalar.copy(
                codes[:].rearrange("p (t c i) -> p c t i", t=PACK, i=4),
                raw[:].rearrange("p (c i t) -> p c t i", t=PACK, i=4),
            )
            return codes

        def deal_scales(name, folded):
            nc.vector.tensor_copy(folded[64:128, 0, :].bitcast(I32), folded[0:64, 1, :].bitcast(I32))
            dealt = tile(name, [P, R], U8)
            nc.vector.tensor_copy(
                dealt[:].rearrange("p (t m) -> p t m", t=PACK), folded[:, 0, :].rearrange("p (m t) -> p t m", t=PACK)
            )
            return dealt

        w2_codes = deal_words("w2_codes", w2_raw)
        w_codes = deal_words("w_codes", w_raw)

        banks = [[psum.tile([P, JH], F32, name=f"a{t}{h}", tag=f"bank{2 * t + h}") for h in range(2)] for t in range(PACK)]

        def a_pass(t, h, codes, plane, words, scale_bytes, first):
            nc.tensor.matmul_mx(
                banks[t][h][:],
                lhsT=codes[:, t * P : (t + 1) * P].bitcast(FP8X4),
                lhsT_scale=plane[:, t * P : (t + 1) * P],
                rhs=words[:, h * JH : (h + 1) * JH].bitcast(FP4X4),
                rhs_scale=scale_bytes,
                start=first,
                stop=not first,
            )

        xo_g = tile("xo_g", [P, J], U16)
        nc.vector.tensor_copy(xo_g[:], xo_win[:].indirect(l2[:]))
        xo_gs = tile("xo_gs", [P, J], U8)
        nc.vector.tensor_copy(xo_gs[:], xo_plane[:].indirect(l2[:]))
        w2_dealt = deal_scales("w2_dealt", w2_fold)

        def note_passes(t):
            for h in range(2):
                a_pass(t, h, w2_codes, w2_dealt, xo_g, xo_gs[:, h * JH : (h + 1) * JH], True)

        for t in range(PACK - 1):
            note_passes(t)

        xt_g = tile("xt_g", [P, J], U16)
        nc.vector.tensor_copy(xt_g[:], xt_win[:].indirect(l1[:]))
        w_dealt = deal_scales("w_dealt", w_fold)
        xt_gs = [tile(f"xt_gs{h}", [P, JH], U8) for h in range(2)]
        for h in range(2):
            nc.vector.tensor_copy(xt_gs[h][:], xt_plane[:].indirect(l1[:, h * JH // 16 : (h + 1) * JH // 16]))

        a_sb = [tile(f"a_sb{t}", [P, J], F32) for t in range(PACK)]
        for t, h in ((0, 0), (1, 0), (0, 1), (1, 1), (2, 0), (2, 1), (3, 0), (3, 1)):
            if (t, h) == (PACK - 1, 0):
                note_passes(t)
            a_pass(t, h, w_codes, w_dealt, xt_g, xt_gs[h][:], False)
            dst = a_sb[t][:, h * JH : (h + 1) * JH]
            if (t, h) in ((0, 0), (1, 0)):
                nc.scalar.copy(dst, banks[t][h][:])
            else:
                nc.vector.tensor_copy(dst, banks[t][h][:])

        wb_codes = tile("wb_codes", [P, N], U32, tag="w2_raw")
        nc.sync.dma_start(wb_codes[:].bitcast(I32), wb_words[0].rearrange("p n t -> p (n t)").bitcast(I32))
        wo_codes = tile("wo_codes", [P, N], U16, tag="w_raw")
        nc.sync.dma_start(wo_codes[:].bitcast(I32), wo_words[0].bitcast(I32))
        wb_plane = tile("wb_plane", [P, N], U8)
        wo_plane = tile("wo_plane", [P, N], U8)
        for t in (wb_plane, wo_plane):
            nc.vector.memset(t[:].bitcast(I32), 0)
        load_plane(nc.sync, wb_plane, wb_scales)
        load_plane(nc.sync, wo_plane, wo_scales)

        results = []
        pages = []
        for h in range(2):
            cols = slice(h * OH // 16, (h + 1) * OH // 16)
            step = 1 + h
            rows_abs = tile(f"rows_abs{h}", [P, PACK * OH], BF16)
            if h == 1:
                late = tile("late", [P, 2, PACK * OH], F32, tag="ga2")
            for t0 in range(0, PACK, step):
                part = slice(t0 * OH, (t0 + step) * OH)
                if h == 0:
                    ga = tile(f"ga{t0}", [P, OH], F32)[:]
                    gb = tile(f"gb{t0}", [P, OH], F32)[:]
                else:
                    ga, gb = late[:, 0, part], late[:, 1, part]
                for e in range(step):
                    t = t0 + e
                    nc.scalar.activation(ga[:, e * OH : (e + 1) * OH], a_sb[t][:].indirect(l3[:, cols]), COPY, scale=sa_sb[:, t : t + 1])
                    nc.scalar.activation(gb[:, e * OH : (e + 1) * OH], a_sb[t][:].indirect(l4[:, cols]), COPY, scale=sb_sb[:, t : t + 1])
                diff = tile(f"diff{h}{t0}", [P, step * OH], F32, tag=("hid0", "hid_codes0")[t0 // 2] if h else None)
                nc.vector.tensor_tensor(diff[:], ga, gb, ALU.subtract)
                nc.vector.scalar_tensor_tensor(rows_abs[:, part], diff[:], -1.0, diff[:], ALU.mult, ALU.max)
            if h == 0:
                for b, tags in enumerate((("w_codes", "w_dealt"), ("ga0", "gb0"))):
                    pages.append([tile(f"page{b}{s}", [P, U], F32, tag=tags[s]) for s in range(2)])
                    for s in range(2):
                        nc.gpsimd.memset(pages[b][s][:], 0.0)
            hid = tile(f"hid{h}", [P, OH * PACK], BF16)
            nc.vector.tensor_copy(
                hid[:].rearrange("p (c i t) -> p c t i", t=PACK, i=4), rows_abs[:].rearrange("p (t c i) -> p c t i", t=PACK, i=4)
            )
            codes = tile(f"hid_codes{h}", [P, OH], U32)
            plane = tile(f"hid_plane{h}", [P, OH], U8)
            nc.vector.quantize_mx(codes[:].bitcast(FP8X4), plane[:], hid[:])
            for b in range(2):
                for s in range(2):
                    rows = slice(b * P, (b + 1) * P)
                    bank = psum.tile([P, OH], F32, name=f"o{h}{b}{s}", tag=f"bank{4 * h + 2 * b + s}")
                    nc.tensor.matmul_mx(
                        bank[:],
                        lhsT=wo_codes[:, rows].bitcast(FP4X4) if s else wb_codes[:, rows].bitcast(FP8X4),
                        lhsT_scale=(wo_plane if s else wb_plane)[:, rows],
                        rhs=codes[:].bitcast(FP8X4),
                        rhs_scale=plane[:],
                        start=True,
                        stop=True,
                    )
                    res = tile(f"res{h}{b}{s}", [P, OH], F32)
                    nc.vector.tensor_copy(res[:], bank[:])
                    results.append((h, b, s, res))

        for h, b, s, res in results:
            cols = slice(h * OH // 16, (h + 1) * OH // 16)
            nc.scalar.activation(pages[b][s][:].indirect((l6 if s else l5)[:, cols]), res[:], COPY)
            if h == 1 and s == 1:
                for c in range(2):
                    part = slice(c * U // 2, (c + 1) * U // 2)
                    y = tile(f"y{b}{c}", [P, U // 2], F32)
                    nc.vector.tensor_tensor(y[:], pages[b][0][:, part], pages[b][1][:, part], ALU.add)
                    (nc.scalar if b == 1 and c == 1 else nc.sync).dma_start(out[b * P : (b + 1) * P, part], y[:])
